import numpy as np
import ml_dtypes


def mxq(x, axis, fmt="e4m3"):
    dtype, down = {"e4m3": (ml_dtypes.float8_e4m3fn, 7), "e5m2": (ml_dtypes.float8_e5m2, 14)}[fmt]
    v = np.moveaxis(np.asarray(x, np.float32).astype(ml_dtypes.bfloat16).astype(np.float64), axis, -1)
    blocks = v.reshape(v.shape[:-1] + (-1, 32))
    amax = np.abs(blocks).max(-1, keepdims=True)
    byte = np.maximum(np.where(amax > 0, np.frexp(amax)[1] - 1 + 127, 0) - down, 1)
    scale = np.exp2(byte - 127.0)
    codes = (blocks / scale).astype(np.float32).astype(dtype).astype(np.float64)
    return np.moveaxis((codes * scale).reshape(v.shape), -1, axis)


WIDE = False


def mx_kscale(k):
    if not WIDE:
        return np.ones(k)
    levels = np.array([10, -10, 5, -5, 0])
    if k % 512:
        return np.exp2(np.random.permutation(np.resize(levels, k // 32))).repeat(32)
    a = np.empty((k // 512, 16))
    for p in range(k // 512):
        a[p, :8] = np.random.permutation(np.resize(levels, 8))
        for g in range(8):
            far = levels[np.abs(levels - a[p, g]) >= 10]
            a[p, g + 8] = far[np.random.randint(len(far))]
    return np.exp2(a.ravel()).repeat(32)


def f64(x):
    return np.asarray(x).astype(np.float64)


def striped(idx):
    return np.tile(idx.reshape(-1, 16).T, (8, 1)).astype(np.uint16)


def unstriped(offs):
    return offs[:16].T.reshape(-1).astype(np.int64)


E2M1 = np.array([0.0, 0.5, 1.0, 1.5, 2.0, 3.0, 4.0, 6.0, -0.0, -0.5, -1.0, -1.5, -2.0, -3.0, -4.0, -6.0])


def pack_weight(w, fmt):
    k, n = w.shape
    w = f64(np.asarray(w, np.float32).astype(ml_dtypes.bfloat16)).reshape(k // 32, 32, n)
    amax = np.abs(w).max(1)
    if fmt == "e4m3":
        byte = np.frexp(amax)[1] - 1 + 127 - 7
    else:
        mant, ex = np.frexp(amax / 6.0)
        byte = np.where(mant > 0.5, ex, ex - 1) + 127
    byte = np.clip(np.where(amax > 0, byte, 1), 1, 254)
    scaled = (w * np.exp2(127.0 - byte)[:, None, :]).reshape(k, n).astype(np.float32)
    by_word = np.ascontiguousarray(scaled.reshape(k // 512, 128, 4, n).transpose(0, 1, 3, 2))
    if fmt == "e4m3":
        words = by_word.astype(ml_dtypes.float8_e4m3fn).view(np.uint8)
    else:
        c = by_word.astype(ml_dtypes.float4_e2m1fn).view(np.uint8) & 0xF
        words = (c[..., 0::2] | (c[..., 1::2] << 4)).reshape(k // 512, 128, 2 * n)
    return np.ascontiguousarray(words), np.ascontiguousarray(byte.astype(np.uint8).reshape(k // 512, 16, n))


def unpack_weight(words, scales, fmt):
    g, _, n = scales.shape
    words = np.ascontiguousarray(words).reshape(g, 128, n, -1)
    if fmt == "e4m3":
        vals = words.view(ml_dtypes.float8_e4m3fn).astype(np.float64)
    else:
        nib = np.empty((g, 128, n, 4), np.uint8)
        nib[..., 0::2] = words & 0xF
        nib[..., 1::2] = words >> 4
        vals = E2M1[nib]
    vals = vals * np.repeat(np.exp2(scales.astype(np.float64) - 127.0), 8, axis=1)[..., None]
    return vals.transpose(0, 1, 3, 2).reshape(g * 512, n)


def silu(v):
    return v / (1.0 + np.exp(-np.maximum(v, -700.0)))


K, T, E, C, H, N = 512, 640, 4, 128, 1024, 256
R = 4


def by_expert(wq, xq):
    return np.concatenate([wq[e].T @ xq[:, e * C:(e + 1) * C] for e in range(E)], axis=1)


def setup_inputs():
    n = np.random.standard_normal
    s = mx_kscale(K)[:, None]
    u = mx_kscale(H)
    slot_token = np.concatenate([r * (T // R) + np.random.permutation(T // R)[:C // R] for e in range(E) for r in range(R)])
    w1 = [pack_weight(m, "e2m1") for m in n((E, K, H)) / np.sqrt(K) / s[None] * u[None, None, :]]
    w2 = [pack_weight(m, "e2m1") for m in n((E, H, N)) / np.sqrt(H) / u[None, :, None]]
    return {
        "xT": (n((K, T)) * s).astype(np.float32),
        "w1_words": np.stack([m[0] for m in w1]),
        "w1_scales": np.stack([m[1] for m in w1]),
        "w2_words": np.stack([m[0] for m in w2]),
        "w2_scales": np.stack([m[1] for m in w2]),
        "offs": striped(slot_token),
    }


def reference(xT, w1_words, w1_scales, w2_words, w2_scales, offs):
    idx = unstriped(offs)
    w1 = np.stack([unpack_weight(w1_words[e], w1_scales[e], "e2m1") for e in range(E)])
    w2 = np.stack([unpack_weight(w2_words[e], w2_scales[e], "e2m1") for e in range(E)])
    xq = mxq(f64(xT)[:, idx], 0, "e4m3")
    h = silu(by_expert(w1, xq))
    y = by_expert(w2, mxq(h, 0, "e4m3"))
    return y.reshape(N, E, R, C // R).transpose(0, 2, 1, 3).reshape(N, E * C)

@@ -1,0 +1,173 @@
+from contextlib import ExitStack
+
+import concourse.mybir as mybir
+
+FLOPS = 805306368
+
+K, T, E, C, H, N = 512, 640, 4, 128, 1024, 256
+R = 4
+P = 128
+G = H // 512
+
+F32 = mybir.dt.float32
+BF16 = mybir.dt.bfloat16
+I32 = mybir.dt.int32
+U32 = mybir.dt.uint32
+U16 = mybir.dt.uint16
+U8 = mybir.dt.uint8
+FP8X4 = mybir.dt.float8_e4m3fn_x4
+FP4X4 = mybir.dt.float4_e2m1fn_x4
+ACT = mybir.ActivationFunctionType
+
+CHUNKS = [(0, 256), (256, 256), (512, 128)]
+CAST_ON_SCALAR = {0, 2}
+
+
+def tile_moe_eps_mlp_silu_kernel(tc, xT, w1_words, w1_scales, w2_words, w2_scales, offs, out):
+    nc = tc.nc
+    with ExitStack() as ctx:
+        keep = ctx.enter_context(tc.tile_pool(name="keep", bufs=1))
+        work = ctx.enter_context(tc.tile_pool(name="work", bufs=4))
+        hp = ctx.enter_context(tc.psum_pool(name="hp", bufs=4))
+        yp = ctx.enter_context(tc.psum_pool(name="yp", bufs=2))
+
+        offsets = keep.tile([P, E * C // 16], U16, name="offsets")
+        raw_scales = keep.tile([P, H], U8, name="raw_scales", align_bytes=64)
+        perm_scales = keep.tile([P, H], U8, name="perm_scales", align_bytes=64)
+        x_codes = keep.tile([P, T], U32, name="x_codes", align_bytes=64)
+        x_bytes = keep.tile([P, T], U8, name="x_bytes", align_bytes=64)
+        w2 = keep.tile([P, E * G, 2 * N], U8, name="w2", align_bytes=64)
+        w2_plane = keep.tile([P, E * G, N], U8, name="w2_plane", align_bytes=64)
+        w1_raw = [keep.tile([P, 2 * H], U8, name=f"w1_raw{e}", align_bytes=64) for e in range(E)]
+        w1 = [keep.tile([P, 2 * H], U8, name=f"w1_{e}", align_bytes=64) for e in range(E)]
+        w1_plane = [perm_scales] + [keep.tile([P, H], U8, name=f"w1_plane{e}", align_bytes=64) for e in range(1, E)]
+        x_raw = [keep.tile([P, 4, w], F32, name=f"x_raw{i}") for i, (c0, w) in enumerate(CHUNKS)]
+        results = keep.tile([P, 2, E * C], F32, name="results")
+        warm = keep.tile([P, 1], F32, name="warm")
+        warm_out = keep.tile([P, 1], F32, name="warm_out")
+
+        nc.vector.memset(raw_scales[:].bitcast(I32), 0)
+        nc.vector.memset(warm[:], 0.0)
+        nc.scalar.activation(warm_out[:], warm[:], ACT.Silu)
+        nc.gpsimd.memset(w2_plane[:].rearrange("p a n -> p (a n)").bitcast(I32), 0)
+        for e in range(1, E):
+            nc.gpsimd.memset(w1_plane[e][:].bitcast(I32), 0)
+        nc.gpsimd.memset(x_bytes[:], 0)
+
+        nc.sync.dma_start(w1_raw[0][:].bitcast(I32), w1_words[0, 0].bitcast(I32))
+        for q in range(4):
+            nc.scalar.dma_start(raw_scales[32 * q : 32 * q + 16, :].bitcast(I32), w1_scales[:, 0, 4 * q : 4 * q + 4, :].bitcast(I32))
+        for i, (c0, w) in enumerate(CHUNKS):
+            nc.sync.dma_start(x_raw[i][:], xT[:, c0 : c0 + w].rearrange("(p j) w -> p j w", j=4))
+        nc.sync.dma_start(offsets[:], offs)
+        for e in range(1, E):
+            nc.sync.dma_start(w1_raw[e][:].bitcast(I32), w1_words[e, 0].bitcast(I32))
+        nc.sync.dma_start(w2[:].bitcast(I32), w2_words.rearrange("e s p b -> p (e s) b").bitcast(I32))
+        for q in range(4):
+            nc.gpsimd.dma_start(
+                w2_plane[32 * q : 32 * q + 4].bitcast(I32),
+                w2_scales[:, :, 4 * q : 4 * q + 4, :].rearrange("e s q n -> q (e s) n").bitcast(I32),
+            )
+
+        def permute_words(e):
+            nc.vector.tensor_copy(
+                w1[e][:].bitcast(U16).rearrange("p (g t m) -> p g t m", g=G, t=4),
+                w1_raw[e][:].bitcast(U16).rearrange("p (g m t) -> p g t m", g=G, t=4),
+            )
+
+        nc.vector.tensor_copy(
+            perm_scales[:].rearrange("p (g t m) -> p g t m", g=G, t=4),
+            raw_scales[:].rearrange("p (g m t) -> p g t m", g=G, t=4),
+        )
+        for e in range(1, E):
+            nc.sync.dma_start(w1_plane[e][0:112, :].bitcast(I32), perm_scales[4 * e : 4 * e + 112, :].bitcast(I32))
+        permute_words(0)
+
+        grouped = {}
+
+        def cast(u):
+            i = 0 if u < 2 else 1 if u < 4 else 2
+            c = u * P - CHUNKS[i][0]
+            grouped[u] = work.tile([P, P, 4], BF16, name=f"grouped{u}", align_bytes=64, bufs=1)
+            src = x_raw[i][:, :, c : c + P].rearrange("p j w -> p w j")
+            if u in CAST_ON_SCALAR:
+                nc.scalar.activation(grouped[u][:], src, ACT.Copy)
+            else:
+                nc.vector.tensor_copy(grouped[u][:], src)
+
+        def quantise(u):
+            cols = slice(u * P, (u + 1) * P)
+            nc.vector.quantize_mx(x_codes[:, cols].bitcast(FP8X4), x_bytes[:, cols], grouped[u][:].rearrange("p w j -> p (w j)"))
+
+        for u in range(5):
+            cast(u)
+        for u in range(5):
+            quantise(u)
+
+        hidden = {}
+
+        def stage_a(e):
+            if e > 0:
+                permute_words(e)
+            lst = offsets[:, 8 * e : 8 * e + 8]
+            s_codes = work.tile([P, C], U32, name="s_codes", align_bytes=64)
+            s_bytes = work.tile([P, C], U8, name="s_bytes", align_bytes=64)
+            nc.vector.tensor_copy(s_codes[:], x_codes[:].indirect(lst))
+            nc.vector.tensor_copy(s_bytes[:], x_bytes[:].indirect(lst))
+            hidden[e] = work.tile([P, G, C, 4], BF16, name="hidden", align_bytes=64)
+            for g in range(G):
+                a = hp.tile([P, 4, C], F32, name="a")
+                for t in range(4):
+                    c = g * 512 + t * P
+                    nc.tensor.matmul_mx(
+                        out=a[:, t, :],
+                        lhsT=w1[e][:, 2 * c : 2 * c + 2 * P].bitcast(FP4X4),
+                        lhsT_scale=w1_plane[e][:, c : c + P],
+                        rhs=s_codes[:].bitcast(FP8X4),
+                        rhs_scale=s_bytes[:],
+                        start=True,
+                        stop=True,
+                    )
+                nc.scalar.activation(hidden[e][:, g], a[:].rearrange("p t n -> p n t"), ACT.Silu)
+
+        def stage_b(e):
+            last = e == E - 1
+            h_codes = work.tile([P, G * C], U32, name="h_codes", align_bytes=64)
+            h_bytes = work.tile([P, G * C], U8, name="h_bytes", align_bytes=64)
+            flat = hidden[e][:].rearrange("p g n t -> p (g n t)")
+            n_q = G if last else 1
+            w = G * C // n_q
+            for k in range(n_q):
+                cols = slice(k * w, (k + 1) * w)
+                nc.vector.quantize_mx(h_codes[:, cols].bitcast(FP8X4), h_bytes[:, cols], flat[:, 4 * k * w : 4 * (k + 1) * w])
+            if last:
+                halves = [yp.tile([P, C], F32, name=f"y{i}", bufs=1)[:] for i in range(2)]
+                order = [(i, g) for g in range(G) for i in range(2)]
+            else:
+                y = yp.tile([P, 2, C], F32, name="y", bufs=2)
+                halves = [y[:, 0, :], y[:, 1, :]]
+                order = [(i, g) for i in range(2) for g in range(G)]
+            for i, g in order:
+                nc.tensor.matmul_mx(
+                    out=halves[i],
+                    lhsT=w2[:, e * G + g, 2 * P * i : 2 * P * i + 2 * P].bitcast(FP4X4),
+                    lhsT_scale=w2_plane[:, e * G + g, P * i : P * i + P],
+                    rhs=h_codes[:, g * C : (g + 1) * C].bitcast(FP8X4),
+                    rhs_scale=h_bytes[:, g * C : (g + 1) * C],
+                    start=(g == 0),
+                    stop=(g == G - 1),
+                )
+            placed = results[:].rearrange("p i (m e u) -> p i m e u", m=R, e=E)[:, :, :, e, :]
+            if last:
+                nc.vector.tensor_copy(placed[:, 0], halves[0].rearrange("p (m u) -> p m u", m=R))
+                nc.scalar.activation(placed[:, 1], halves[1].rearrange("p (m u) -> p m u", m=R), ACT.Copy)
+            else:
+                nc.scalar.activation(placed, y[:].rearrange("p i (m u) -> p i m u", m=R), ACT.Copy)
+
+        stage_a(0)
+        for e in range(1, E):
+            stage_a(e)
+            stage_b(e - 1)
+        stage_b(E - 1)
+        for i in range(2):
+            nc.sync.dma_start(out[i * P : (i + 1) * P, :], results[:, i, :])

@@ -20,7 +20,7 @@ FP4X4 = mybir.dt.float4_e2m1fn_x4
 ACT = mybir.ActivationFunctionType
 
 CHUNKS = [(0, 256), (256, 256), (512, 128)]
-CAST_ON_SCALAR = {0, 2}
+CAST_ON_SCALAR = {0, 2, 3}
 
 
 def tile_moe_eps_mlp_silu_kernel(tc, xT, w1_words, w1_scales, w2_words, w2_scales, offs, out):
@@ -36,38 +36,32 @@ def tile_moe_eps_mlp_silu_kernel(tc, xT, w1_words, w1_scales, w2_words, w2_scale
         perm_scales = keep.tile([P, H], U8, name="perm_scales", align_bytes=64)
         x_codes = keep.tile([P, T], U32, name="x_codes", align_bytes=64)
         x_bytes = keep.tile([P, T], U8, name="x_bytes", align_bytes=64)
-        w2 = keep.tile([P, E * G, 2 * N], U8, name="w2", align_bytes=64)
         w2_plane = keep.tile([P, E * G, N], U8, name="w2_plane", align_bytes=64)
-        w1_raw = [keep.tile([P, 2 * H], U8, name=f"w1_raw{e}", align_bytes=64) for e in range(E)]
+        w1_raw = [keep.tile([P, 2 * H], U8, name=f"w1_raw{e}", tag=f"w1_raw{e}", align_bytes=64) for e in range(E - 1)]
         w1 = [keep.tile([P, 2 * H], U8, name=f"w1_{e}", align_bytes=64) for e in range(E)]
         w1_plane = [perm_scales] + [keep.tile([P, H], U8, name=f"w1_plane{e}", align_bytes=64) for e in range(1, E)]
-        x_raw = [keep.tile([P, 4, w], F32, name=f"x_raw{i}") for i, (c0, w) in enumerate(CHUNKS)]
-        results = keep.tile([P, 2, E * C], F32, name="results")
+        x_raw = [keep.tile([P, 4, w], F32, name=f"x_raw{i}", tag=f"x_raw{i}", align_bytes=64) for i, (c0, w) in enumerate(CHUNKS)]
+        results = [keep.tile([P, E * C], F32, name=f"results{i}") for i in range(2)]
         warm = keep.tile([P, 1], F32, name="warm")
         warm_out = keep.tile([P, 1], F32, name="warm_out")
 
         nc.vector.memset(raw_scales[:].bitcast(I32), 0)
         nc.vector.memset(warm[:], 0.0)
         nc.scalar.activation(warm_out[:], warm[:], ACT.Silu)
-        nc.gpsimd.memset(w2_plane[:].rearrange("p a n -> p (a n)").bitcast(I32), 0)
+        nc.vector.memset(w2_plane[:].rearrange("p a n -> p (a n)").bitcast(I32), 0)
         for e in range(1, E):
-            nc.gpsimd.memset(w1_plane[e][:].bitcast(I32), 0)
+            nc.vector.memset(w1_plane[e][:].bitcast(I32), 0)
         nc.gpsimd.memset(x_bytes[:], 0)
 
-        nc.sync.dma_start(w1_raw[0][:].bitcast(I32), w1_words[0, 0].bitcast(I32))
         for q in range(4):
             nc.scalar.dma_start(raw_scales[32 * q : 32 * q + 16, :].bitcast(I32), w1_scales[:, 0, 4 * q : 4 * q + 4, :].bitcast(I32))
         for i, (c0, w) in enumerate(CHUNKS):
             nc.sync.dma_start(x_raw[i][:], xT[:, c0 : c0 + w].rearrange("(p j) w -> p j w", j=4))
+            if i == 0:
+                nc.sync.dma_start(w1_raw[0][:].bitcast(I32), w1_words[0, 0].bitcast(I32))
         nc.sync.dma_start(offsets[:], offs)
-        for e in range(1, E):
+        for e in range(1, E - 1):
             nc.sync.dma_start(w1_raw[e][:].bitcast(I32), w1_words[e, 0].bitcast(I32))
-        nc.sync.dma_start(w2[:].bitcast(I32), w2_words.rearrange("e s p b -> p (e s) b").bitcast(I32))
-        for q in range(4):
-            nc.gpsimd.dma_start(
-                w2_plane[32 * q : 32 * q + 4].bitcast(I32),
-                w2_scales[:, :, 4 * q : 4 * q + 4, :].rearrange("e s q n -> q (e s) n").bitcast(I32),
-            )
 
         def permute_words(e):
             nc.vector.tensor_copy(
@@ -79,8 +73,10 @@ def tile_moe_eps_mlp_silu_kernel(tc, xT, w1_words, w1_scales, w2_words, w2_scale
             perm_scales[:].rearrange("p (g t m) -> p g t m", g=G, t=4),
             raw_scales[:].rearrange("p (g m t) -> p g t m", g=G, t=4),
         )
-        for e in range(1, E):
+        def move_scales(e):
             nc.sync.dma_start(w1_plane[e][0:112, :].bitcast(I32), perm_scales[4 * e : 4 * e + 112, :].bitcast(I32))
+
+        move_scales(1)
         permute_words(0)
 
         grouped = {}
@@ -99,12 +95,27 @@ def tile_moe_eps_mlp_silu_kernel(tc, xT, w1_words, w1_scales, w2_words, w2_scale
             cols = slice(u * P, (u + 1) * P)
             nc.vector.quantize_mx(x_codes[:, cols].bitcast(FP8X4), x_bytes[:, cols], grouped[u][:].rearrange("p w j -> p (w j)"))
 
-        for u in range(5):
+        cast(0)
+        cast(1)
+        w2 = keep.tile([P, E * G, 2 * N], U8, name="w2", tag="x_raw0", align_bytes=64)
+        nc.sync.dma_start(w2[:].bitcast(I32), w2_words.rearrange("e s p b -> p (e s) b").bitcast(I32))
+        w1_raw.append(keep.tile([P, 2 * H], U8, name="w1_raw3", tag="w1_raw0", align_bytes=64))
+        nc.sync.dma_start(w1_raw[3][:].bitcast(I32), w1_words[3, 0].bitcast(I32))
+        for q in range(4):
+            nc.sync.dma_start(
+                w2_plane[32 * q : 32 * q + 4].bitcast(I32),
+                w2_scales[:, :, 4 * q : 4 * q + 4, :].rearrange("e s q n -> q (e s) n").bitcast(I32),
+            )
+        move_scales(2)
+        move_scales(3)
+        quantise(0)
+        quantise(1)
+        for u in range(2, 5):
             cast(u)
-        for u in range(5):
+        for u in range(2, 5):
             quantise(u)
 
-        hidden = {}
+        hq = {}
 
         def stage_a(e):
             if e > 0:
@@ -114,7 +125,6 @@ def tile_moe_eps_mlp_silu_kernel(tc, xT, w1_words, w1_scales, w2_words, w2_scale
             s_bytes = work.tile([P, C], U8, name="s_bytes", align_bytes=64)
             nc.vector.tensor_copy(s_codes[:], x_codes[:].indirect(lst))
             nc.vector.tensor_copy(s_bytes[:], x_bytes[:].indirect(lst))
-            hidden[e] = work.tile([P, G, C, 4], BF16, name="hidden", align_bytes=64)
             for g in range(G):
                 a = hp.tile([P, 4, C], F32, name="a")
                 for t in range(4):
@@ -128,41 +138,31 @@ def tile_moe_eps_mlp_silu_kernel(tc, xT, w1_words, w1_scales, w2_words, w2_scale
                         start=True,
                         stop=True,
                     )
-                nc.scalar.activation(hidden[e][:, g], a[:].rearrange("p t n -> p n t"), ACT.Silu)
+                h = work.tile([P, C, 4], BF16, name="h", align_bytes=64)
+                nc.scalar.activation(h[:], a[:].rearrange("p t n -> p n t"), ACT.Silu)
+                hq[e, g] = h
 
         def stage_b(e):
-            last = e == E - 1
-            h_codes = work.tile([P, G * C], U32, name="h_codes", align_bytes=64)
-            h_bytes = work.tile([P, G * C], U8, name="h_bytes", align_bytes=64)
-            flat = hidden[e][:].rearrange("p g n t -> p (g n t)")
-            n_q = G if last else 1
-            w = G * C // n_q
-            for k in range(n_q):
-                cols = slice(k * w, (k + 1) * w)
-                nc.vector.quantize_mx(h_codes[:, cols].bitcast(FP8X4), h_bytes[:, cols], flat[:, 4 * k * w : 4 * (k + 1) * w])
-            if last:
-                halves = [yp.tile([P, C], F32, name=f"y{i}", bufs=1)[:] for i in range(2)]
-                order = [(i, g) for g in range(G) for i in range(2)]
-            else:
-                y = yp.tile([P, 2, C], F32, name="y", bufs=2)
-                halves = [y[:, 0, :], y[:, 1, :]]
-                order = [(i, g) for i in range(2) for g in range(G)]
-            for i, g in order:
-                nc.tensor.matmul_mx(
-                    out=halves[i],
-                    lhsT=w2[:, e * G + g, 2 * P * i : 2 * P * i + 2 * P].bitcast(FP4X4),
-                    lhsT_scale=w2_plane[:, e * G + g, P * i : P * i + P],
-                    rhs=h_codes[:, g * C : (g + 1) * C].bitcast(FP8X4),
-                    rhs_scale=h_bytes[:, g * C : (g + 1) * C],
-                    start=(g == 0),
-                    stop=(g == G - 1),
+            y = [yp.tile([P, C], F32, name=f"y{i}") for i in range(2)]
+            for g in range(G):
+                h_codes = work.tile([P, C], U32, name="h_codes", align_bytes=64)
+                h_bytes = work.tile([P, C], U8, name="h_bytes", align_bytes=64)
+                nc.vector.quantize_mx(h_codes[:].bitcast(FP8X4), h_bytes[:], hq[e, g][:].rearrange("p n t -> p (n t)"))
+                for i in range(2):
+                    nc.tensor.matmul_mx(
+                        out=y[i][:],
+                        lhsT=w2[:, e * G + g, 2 * P * i : 2 * P * i + 2 * P].bitcast(FP4X4),
+                        lhsT_scale=w2_plane[:, e * G + g, P * i : P * i + P],
+                        rhs=h_codes[:].bitcast(FP8X4),
+                        rhs_scale=h_bytes[:],
+                        start=(g == 0),
+                        stop=(g == G - 1),
+                    )
+            for i in range(2):
+                nc.vector.tensor_copy(
+                    results[i][:].rearrange("p (m e u) -> p m e u", m=R, e=E)[:, :, e, :],
+                    y[i][:].rearrange("p (m u) -> p m u", m=R),
                 )
-            placed = results[:].rearrange("p i (m e u) -> p i m e u", m=R, e=E)[:, :, :, e, :]
-            if last:
-                nc.vector.tensor_copy(placed[:, 0], halves[0].rearrange("p (m u) -> p m u", m=R))
-                nc.scalar.activation(placed[:, 1], halves[1].rearrange("p (m u) -> p m u", m=R), ACT.Copy)
-            else:
-                nc.scalar.activation(placed, y[:].rearrange("p i (m u) -> p i m u", m=R), ACT.Copy)
 
         stage_a(0)
         for e in range(1, E):
@@ -170,4 +170,4 @@ def tile_moe_eps_mlp_silu_kernel(tc, xT, w1_words, w1_scales, w2_words, w2_scale
             stage_b(e - 1)
         stage_b(E - 1)
         for i in range(2):
-            nc.sync.dma_start(out[i * P : (i + 1) * P, :], results[:, i, :])
+            nc.sync.dma_start(out[i * P : (i + 1) * P, :], results[i][:])

from contextlib import ExitStack

import concourse.mybir as mybir

FLOPS = 805306368

K, T, E, C, H, N = 512, 640, 4, 128, 1024, 256
R = 4
P = 128
G = H // 512

F32 = mybir.dt.float32
BF16 = mybir.dt.bfloat16
I32 = mybir.dt.int32
U32 = mybir.dt.uint32
U16 = mybir.dt.uint16
U8 = mybir.dt.uint8
FP8X4 = mybir.dt.float8_e4m3fn_x4
FP4X4 = mybir.dt.float4_e2m1fn_x4
ACT = mybir.ActivationFunctionType

CHUNKS = [(0, 256), (256, 256), (512, 128)]
CAST_ON_SCALAR = {0, 2, 3}


def tile_moe_eps_mlp_silu_kernel(tc, xT, w1_words, w1_scales, w2_words, w2_scales, offs, out):
    nc = tc.nc
    with ExitStack() as ctx:
        keep = ctx.enter_context(tc.tile_pool(name="keep", bufs=1))
        work = ctx.enter_context(tc.tile_pool(name="work", bufs=4))
        hp = ctx.enter_context(tc.psum_pool(name="hp", bufs=4))
        yp = ctx.enter_context(tc.psum_pool(name="yp", bufs=2))

        offsets = keep.tile([P, E * C // 16], U16, name="offsets")
        raw_scales = keep.tile([P, H], U8, name="raw_scales", align_bytes=64)
        perm_scales = keep.tile([P, H], U8, name="perm_scales", align_bytes=64)
        x_codes = keep.tile([P, T], U32, name="x_codes", align_bytes=64)
        x_bytes = keep.tile([P, T], U8, name="x_bytes", align_bytes=64)
        w2_plane = keep.tile([P, E * G, N], U8, name="w2_plane", align_bytes=64)
        w1_raw = [keep.tile([P, 2 * H], U8, name=f"w1_raw{e}", tag=f"w1_raw{e}", align_bytes=64) for e in range(E - 1)]
        w1 = [keep.tile([P, 2 * H], U8, name=f"w1_{e}", align_bytes=64) for e in range(E)]
        w1_plane = [perm_scales] + [keep.tile([P, H], U8, name=f"w1_plane{e}", align_bytes=64) for e in range(1, E)]
        x_raw = [keep.tile([P, 4, w], F32, name=f"x_raw{i}", tag=f"x_raw{i}", align_bytes=64) for i, (c0, w) in enumerate(CHUNKS)]
        results = [keep.tile([P, E * C], F32, name=f"results{i}") for i in range(2)]
        warm = keep.tile([P, 1], F32, name="warm")
        warm_out = keep.tile([P, 1], F32, name="warm_out")

        nc.vector.memset(raw_scales[:].bitcast(I32), 0)
        nc.vector.memset(warm[:], 0.0)
        nc.scalar.activation(warm_out[:], warm[:], ACT.Silu)
        nc.vector.memset(w2_plane[:].rearrange("p a n -> p (a n)").bitcast(I32), 0)
        for e in range(1, E):
            nc.vector.memset(w1_plane[e][:].bitcast(I32), 0)
        nc.gpsimd.memset(x_bytes[:], 0)

        for q in range(4):
            nc.scalar.dma_start(raw_scales[32 * q : 32 * q + 16, :].bitcast(I32), w1_scales[:, 0, 4 * q : 4 * q + 4, :].bitcast(I32))
        for i, (c0, w) in enumerate(CHUNKS):
            nc.sync.dma_start(x_raw[i][:], xT[:, c0 : c0 + w].rearrange("(p j) w -> p j w", j=4))
            if i == 0:
                nc.sync.dma_start(w1_raw[0][:].bitcast(I32), w1_words[0, 0].bitcast(I32))
        nc.sync.dma_start(offsets[:], offs)
        for e in range(1, E - 1):
            nc.sync.dma_start(w1_raw[e][:].bitcast(I32), w1_words[e, 0].bitcast(I32))

        def permute_words(e):
            nc.vector.tensor_copy(
                w1[e][:].bitcast(U16).rearrange("p (g t m) -> p g t m", g=G, t=4),
                w1_raw[e][:].bitcast(U16).rearrange("p (g m t) -> p g t m", g=G, t=4),
            )

        nc.vector.tensor_copy(
            perm_scales[:].rearrange("p (g t m) -> p g t m", g=G, t=4),
            raw_scales[:].rearrange("p (g m t) -> p g t m", g=G, t=4),
        )
        def move_scales(e):
            nc.sync.dma_start(w1_plane[e][0:112, :].bitcast(I32), perm_scales[4 * e : 4 * e + 112, :].bitcast(I32))

        move_scales(1)
        permute_words(0)

        grouped = {}

        def cast(u):
            i = 0 if u < 2 else 1 if u < 4 else 2
            c = u * P - CHUNKS[i][0]
            grouped[u] = work.tile([P, P, 4], BF16, name=f"grouped{u}", align_bytes=64, bufs=1)
            src = x_raw[i][:, :, c : c + P].rearrange("p j w -> p w j")
            if u in CAST_ON_SCALAR:
                nc.scalar.activation(grouped[u][:], src, ACT.Copy)
            else:
                nc.vector.tensor_copy(grouped[u][:], src)

        def quantise(u):
            cols = slice(u * P, (u + 1) * P)
            nc.vector.quantize_mx(x_codes[:, cols].bitcast(FP8X4), x_bytes[:, cols], grouped[u][:].rearrange("p w j -> p (w j)"))

        cast(0)
        cast(1)
        w2 = keep.tile([P, E * G, 2 * N], U8, name="w2", tag="x_raw0", align_bytes=64)
        nc.sync.dma_start(w2[:].bitcast(I32), w2_words.rearrange("e s p b -> p (e s) b").bitcast(I32))
        w1_raw.append(keep.tile([P, 2 * H], U8, name="w1_raw3", tag="w1_raw0", align_bytes=64))
        nc.sync.dma_start(w1_raw[3][:].bitcast(I32), w1_words[3, 0].bitcast(I32))
        for q in range(4):
            nc.sync.dma_start(
                w2_plane[32 * q : 32 * q + 4].bitcast(I32),
                w2_scales[:, :, 4 * q : 4 * q + 4, :].rearrange("e s q n -> q (e s) n").bitcast(I32),
            )
        move_scales(2)
        move_scales(3)
        quantise(0)
        quantise(1)
        for u in range(2, 5):
            cast(u)
        for u in range(2, 5):
            quantise(u)

        hq = {}

        def stage_a(e):
            if e > 0:
                permute_words(e)
            lst = offsets[:, 8 * e : 8 * e + 8]
            s_codes = work.tile([P, C], U32, name="s_codes", align_bytes=64)
            s_bytes = work.tile([P, C], U8, name="s_bytes", align_bytes=64)
            nc.vector.tensor_copy(s_codes[:], x_codes[:].indirect(lst))
            nc.vector.tensor_copy(s_bytes[:], x_bytes[:].indirect(lst))
            for g in range(G):
                a = hp.tile([P, 4, C], F32, name="a")
                for t in range(4):
                    c = g * 512 + t * P
                    nc.tensor.matmul_mx(
                        out=a[:, t, :],
                        lhsT=w1[e][:, 2 * c : 2 * c + 2 * P].bitcast(FP4X4),
                        lhsT_scale=w1_plane[e][:, c : c + P],
                        rhs=s_codes[:].bitcast(FP8X4),
                        rhs_scale=s_bytes[:],
                        start=True,
                        stop=True,
                    )
                h = work.tile([P, C, 4], BF16, name="h", align_bytes=64)
                nc.scalar.activation(h[:], a[:].rearrange("p t n -> p n t"), ACT.Silu)
                hq[e, g] = h

        def stage_b(e):
            y = [yp.tile([P, C], F32, name=f"y{i}") for i in range(2)]
            for g in range(G):
                h_codes = work.tile([P, C], U32, name="h_codes", align_bytes=64)
                h_bytes = work.tile([P, C], U8, name="h_bytes", align_bytes=64)
                nc.vector.quantize_mx(h_codes[:].bitcast(FP8X4), h_bytes[:], hq[e, g][:].rearrange("p n t -> p (n t)"))
                for i in range(2):
                    nc.tensor.matmul_mx(
                        out=y[i][:],
                        lhsT=w2[:, e * G + g, 2 * P * i : 2 * P * i + 2 * P].bitcast(FP4X4),
                        lhsT_scale=w2_plane[:, e * G + g, P * i : P * i + P],
                        rhs=h_codes[:].bitcast(FP8X4),
                        rhs_scale=h_bytes[:],
                        start=(g == 0),
                        stop=(g == G - 1),
                    )
            for i in range(2):
                nc.vector.tensor_copy(
                    results[i][:].rearrange("p (m e u) -> p m e u", m=R, e=E)[:, :, e, :],
                    y[i][:].rearrange("p (m u) -> p m u", m=R),
                )

        stage_a(0)
        for e in range(1, E):
            stage_a(e)
            stage_b(e - 1)
        stage_b(E - 1)
        for i in range(2):
            nc.sync.dma_start(out[i * P : (i + 1) * P, :], results[i][:])
